import numpy as np
import ml_dtypes


def mxq(x, axis, fmt="e4m3"):
    dtype, down = {"e4m3": (ml_dtypes.float8_e4m3fn, 7), "e5m2": (ml_dtypes.float8_e5m2, 14)}[fmt]
    v = np.moveaxis(np.asarray(x, np.float32).astype(ml_dtypes.bfloat16).astype(np.float64), axis, -1)
    blocks = v.reshape(v.shape[:-1] + (-1, 32))
    amax = np.abs(blocks).max(-1, keepdims=True)
    byte = np.maximum(np.where(amax > 0, np.frexp(amax)[1] - 1 + 127, 0) - down, 1)
    scale = np.exp2(byte - 127.0)
    codes = (blocks / scale).astype(np.float32).astype(dtype).astype(np.float64)
    return np.moveaxis((codes * scale).reshape(v.shape), -1, axis)


WIDE = False


def mx_kscale(k):
    if not WIDE:
        return np.ones(k)
    levels = np.array([10, -10, 5, -5, 0])
    if k % 512:
        return np.exp2(np.random.permutation(np.resize(levels, k // 32))).repeat(32)
    a = np.empty((k // 512, 16))
    for p in range(k // 512):
        a[p, :8] = np.random.permutation(np.resize(levels, 8))
        for g in range(8):
            far = levels[np.abs(levels - a[p, g]) >= 10]
            a[p, g + 8] = far[np.random.randint(len(far))]
    return np.exp2(a.ravel()).repeat(32)


def f64(x):
    return np.asarray(x).astype(np.float64)


def striped(idx):
    return np.tile(np.asarray(idx).reshape(-1, 16).T, (8, 1)).astype(np.uint16)


def unstriped(offs):
    return offs[:16].T.reshape(-1).astype(np.int64)


E2M1 = np.array([0.0, 0.5, 1.0, 1.5, 2.0, 3.0, 4.0, 6.0, -0.0, -0.5, -1.0, -1.5, -2.0, -3.0, -4.0, -6.0])


def pack_weight(w, fmt):
    k, n = w.shape
    w = f64(np.asarray(w, np.float32).astype(ml_dtypes.bfloat16)).reshape(k // 32, 32, n)
    amax = np.abs(w).max(1)
    if fmt == "e4m3":
        byte = np.frexp(amax)[1] - 1 + 127 - 7
    else:
        mant, ex = np.frexp(amax / 6.0)
        byte = np.where(mant > 0.5, ex, ex - 1) + 127
    byte = np.clip(np.where(amax > 0, byte, 1), 1, 254)
    scaled = (w * np.exp2(127.0 - byte)[:, None, :]).reshape(k, n).astype(np.float32)
    by_word = np.ascontiguousarray(scaled.reshape(k // 512, 128, 4, n).transpose(0, 1, 3, 2))
    if fmt == "e4m3":
        words = by_word.astype(ml_dtypes.float8_e4m3fn).view(np.uint8)
    else:
        c = by_word.astype(ml_dtypes.float4_e2m1fn).view(np.uint8) & 0xF
        words = (c[..., 0::2] | (c[..., 1::2] << 4)).reshape(k // 512, 128, 2 * n)
    return np.ascontiguousarray(words), np.ascontiguousarray(byte.astype(np.uint8).reshape(k // 512, 16, n))


def unpack_weight(words, scales, fmt):
    g, _, n = scales.shape
    words = np.ascontiguousarray(words).reshape(g, 128, n, -1)
    if fmt == "e4m3":
        vals = words.view(ml_dtypes.float8_e4m3fn).astype(np.float64)
    else:
        nib = np.empty((g, 128, n, 4), np.uint8)
        nib[..., 0::2] = words & 0xF
        nib[..., 1::2] = words >> 4
        vals = E2M1[nib]
    vals = vals * np.repeat(np.exp2(scales.astype(np.float64) - 127.0), 8, axis=1)[..., None]
    return vals.transpose(0, 1, 3, 2).reshape(g * 512, n)


def softplus(v):
    return np.log(1.0 + np.exp(v))


K, L, T, C, J = 1024, 512, 256, 1024, 512


def setup_inputs():
    n = np.random.standard_normal
    idx = np.random.permutation(C)[:J]
    fk = mx_kscale(K)
    fl = mx_kscale(L)
    xtp = pack_weight(n((K, T)) / fk[:, None], "e4m3")
    xsp = pack_weight(n((L, T)) / fl[:, None], "e2m1")
    wsp = pack_weight(n((L, J)) * 1 / np.sqrt(L) * fl[:, None], "e4m3")
    return {
        "xt_words": xtp[0],
        "xt_scales": xtp[1],
        "wc": (n((K, C)) * 1 / np.sqrt(K) * fk[:, None]).astype(np.float32),
        "xs_words": xsp[0],
        "xs_scales": xsp[1],
        "ws_words": wsp[0],
        "ws_scales": wsp[1],
        "offs": striped(idx),
    }


def reference(xt_words, xt_scales, wc, xs_words, xs_scales, ws_words, ws_scales, offs):
    idx = unstriped(offs)
    xtu = unpack_weight(xt_words, xt_scales, "e4m3")
    xsu = unpack_weight(xs_words, xs_scales, "e2m1")
    wsu = unpack_weight(ws_words, ws_scales, "e4m3")
    wcq = mxq(f64(wc), 0, "e4m3")
    z = xtu.T @ wcq
    s = xsu.T @ wsu
    y = softplus(np.max(z, axis=1, keepdims=True) - z[:, idx]) - 0.5 * s
    return y

@@ -1,0 +1,195 @@
+from contextlib import ExitStack
+
+import concourse.mybir as mybir
+
+K, L, T, C, J = 1024, 512, 256, 1024, 512
+FLOPS = 2 * T * (K * C + L * J)
+
+F32 = mybir.dt.float32
+BF16 = mybir.dt.bfloat16
+I32 = mybir.dt.int32
+U32 = mybir.dt.uint32
+U16 = mybir.dt.uint16
+U8 = mybir.dt.uint8
+FP8X4 = mybir.dt.float8_e4m3fn_x4
+FP4X4 = mybir.dt.float4_e2m1fn_x4
+ALU = mybir.AluOpType
+ACT = mybir.ActivationFunctionType
+
+P = 128
+PACK = 4
+K_PASS = P * PACK
+PASSES = K // K_PASS
+TILES = T // P
+QUADRANTS = 4
+LINE = 4
+
+PIECES = ((0, 0, 256, 208), (1, 0, 256, 208), (0, 256, 256, 208), (1, 256, 256, 208), (0, 512, 256, 208), (1, 512, 256, 192), (0, 768, 128, 128), (1, 768, 128, 128), (0, 896, 128, 128), (1, 896, 128, 64))
+BLOCKS = ((0, 256), (256, 256), (512, 256), (768, 128), (896, 128))
+GATHERS = ((0, 0, 512), (1, 0, 256), (1, 256, 512))
+OUTS = ((0, 0, 256), (0, 256, 512), (1, 0, 256), (1, 256, 512))
+
+
+def load_scale_rows(queue, plane, scales):
+    for q in range(QUADRANTS):
+        queue.dma_start(
+            out=plane[32 * q : 32 * q + 4, :, :].bitcast(I32),
+            in_=scales[:, 4 * q : 4 * q + 4, :].rearrange("z r c -> r z c").bitcast(I32),
+        )
+
+
+def tile_list_runner_up_gap_kernel(tc, xt_words, xt_scales, wc, xs_words, xs_scales, ws_words, ws_scales, offs, out):
+    nc = tc.nc
+    with ExitStack() as ctx:
+        keep = ctx.enter_context(tc.tile_pool(name="keep", bufs=1))
+        zpsum = ctx.enter_context(tc.psum_pool(name="zpsum", bufs=3))
+        spsum = ctx.enter_context(tc.psum_pool(name="spsum", bufs=1))
+
+        offsets = keep.tile([P, J // 16], U16, name="offsets")
+        xt_codes = keep.tile([P, PASSES, T], U32, name="xt_codes", align_bytes=64)
+        xt_plane = keep.tile([P, PASSES, T], U8, name="xt_plane", align_bytes=64)
+        xs_codes = keep.tile([P, 2 * T], U8, name="xs_codes", align_bytes=64)
+        xs_plane = keep.tile([P, 1, T], U8, name="xs_plane", align_bytes=64)
+        ws_codes = keep.tile([P, J], U32, name="ws_codes", align_bytes=64)
+        ws_plane = keep.tile([P, 1, J], U8, name="ws_plane", align_bytes=64)
+        nc.gpsimd.memset(xt_plane[:].bitcast(U32), 0)
+        for plane in (xs_plane, ws_plane):
+            nc.vector.memset(plane[:].bitcast(U32), 0)
+
+        raw = []
+        for n, (g, c0, width, share) in enumerate(PIECES):
+            piece = keep.tile([P, PACK, width], F32, name="raw%d" % n)
+            rows = wc[g * K_PASS : (g + 1) * K_PASS, c0 : c0 + width]
+            nc.sync.dma_start(out=piece[:], in_=rows.rearrange("(p j) c -> p j c", j=PACK))
+            raw.append(piece)
+            if n == 0:
+                load_scale_rows(nc.sync, xt_plane, xt_scales)
+                nc.sync.dma_start(
+                    out=xt_codes[:].bitcast(I32),
+                    in_=xt_words.rearrange("z p c r -> p z (c r)").bitcast(I32),
+                )
+        nc.sync.dma_start(offsets[:], offs)
+        nc.sync.dma_start(
+            out=ws_codes[:].bitcast(I32), in_=ws_words[0].rearrange("p c r -> p (c r)").bitcast(I32)
+        )
+        nc.sync.dma_start(out=xs_codes[:].bitcast(I32), in_=xs_words[0].bitcast(I32))
+        load_scale_rows(nc.sync, ws_plane, ws_scales)
+        load_scale_rows(nc.sync, xs_plane, xs_scales)
+
+        z = [keep.tile([P, C], F32, name="z%d" % t) for t in range(TILES)]
+        best = [None] * TILES
+        banks = {}
+        grouped = {}
+
+        def cast(n):
+            g, c0, width, share = PIECES[n]
+            grouped[n] = keep.tile([P, width, PACK], BF16, name="grouped%d" % n, align_bytes=64)
+            for first, last, on_scalar in ((0, share, True), (share, width, False)):
+                if first == last:
+                    continue
+                dst = grouped[n][:, first:last, :].rearrange("p (c i) j -> p c j i", i=LINE)
+                src = raw[n][:, :, first:last].rearrange("p j (c i) -> p c j i", i=LINE)
+                if on_scalar:
+                    nc.scalar.activation(out=dst, in_=src, func=ACT.Copy)
+                else:
+                    nc.vector.tensor_copy(out=dst, in_=src)
+
+        def multiply(n):
+            g, c0, width, share = PIECES[n]
+            codes = keep.tile([P, width], U32, name="codes%d" % n, align_bytes=64)
+            plane = keep.tile([P, width], U8, name="plane%d" % n, align_bytes=64)
+            nc.vector.quantize_mx(
+                out=codes[:].bitcast(FP8X4),
+                scales=plane[:],
+                in_=grouped[n][:].rearrange("p c j -> p (c j)"),
+            )
+            for b0, bw in BLOCKS:
+                if b0 < c0 or b0 + bw > c0 + width:
+                    continue
+                for t in range(TILES):
+                    if g == 0:
+                        if b0 + bw == C:
+                            banks[b0, t] = spsum.tile([P, bw], F32, name="last%d" % t, tag="late%d" % t)
+                        else:
+                            banks[b0, t] = zpsum.tile([P, bw], F32, name="zbank%d" % t)
+                    cols = slice(b0 - c0, b0 - c0 + bw)
+                    tokens = slice(t * P, (t + 1) * P)
+                    nc.tensor.matmul_mx(
+                        out=banks[b0, t][:],
+                        lhsT=xt_codes[:, g, tokens].bitcast(FP8X4),
+                        lhsT_scale=xt_plane[:, g, tokens],
+                        rhs=codes[:, cols].bitcast(FP8X4),
+                        rhs_scale=plane[:, cols],
+                        start=(g == 0),
+                        stop=(g == PASSES - 1),
+                    )
+
+        def empty(n):
+            g, c0, width, share = PIECES[n]
+            if g != PASSES - 1:
+                return
+            for b0, bw in BLOCKS:
+                if b0 < c0 or b0 + bw > c0 + width:
+                    continue
+                for t in range(TILES):
+                    running = keep.tile([P, 1], F32, name="best%d_%d" % (b0, t))
+                    nc.vector.tensor_scalar(
+                        out=z[t][:, b0 : b0 + bw],
+                        in0=banks[b0, t][:],
+                        scalar1=1.0,
+                        scalar2=None if best[t] is None else best[t][:],
+                        op0=ALU.mult,
+                        op1=ALU.max,
+                        accum_out=running[:],
+                    )
+                    best[t] = running
+
+        count = len(PIECES)
+        for n in range(count):
+            cast(n)
+            multiply(n)
+            if 1 <= n < count - 2:
+                empty(n - 1)
+        empty(count - 3)
+        empty(count - 1)
+
+        s = [spsum.tile([P, J], F32, name="s%d" % t, tag="late%d" % t) for t in range(TILES)]
+        for t in range(TILES):
+            nc.tensor.matmul_mx(
+                out=s[t][:],
+                lhsT=xs_codes[:, 2 * t * P : 2 * (t + 1) * P].bitcast(FP4X4),
+                lhsT_scale=xs_plane[:, 0, t * P : (t + 1) * P],
+                rhs=ws_codes[:].bitcast(FP8X4),
+                rhs_scale=ws_plane[:, 0, :],
+                start=True,
+                stop=True,
+            )
+
+        negated = keep.tile([P, TILES], F32, name="negated", tag="handover")
+        picked = keep.tile([P, TILES, J], F32, name="picked")
+        decay = keep.tile([P, TILES, J], F32, name="decay")
+        linear = keep.tile([P, TILES, J], F32, name="linear")
+        result = keep.tile([P, TILES, J], F32, name="result")
+        for t in range(TILES):
+            nc.scalar.activation(out=negated[:, t : t + 1], in_=best[t][:], func=ACT.Copy, scale=-1.0)
+        for t, j0, j1 in GATHERS:
+            nc.vector.tensor_copy(picked[:, t, j0:j1], z[t][:].indirect(offsets[:, j0 // 16 : j1 // 16]))
+            nc.scalar.activation(
+                out=decay[:, t, j0:j1], in_=picked[:, t, j0:j1], func=ACT.Exp, bias=negated[:, t : t + 1]
+            )
+        for t in range(TILES):
+            nc.vector.scalar_tensor_tensor(
+                out=linear[:, t, :], in0=s[t][:], scalar=-0.5, in1=picked[:, t, :], op0=ALU.mult, op1=ALU.subtract
+            )
+        logs = keep.tile([P, TILES, J], F32, name="logs", tag="handover")
+        for t, j0, j1 in OUTS:
+            nc.scalar.activation(out=logs[:, t, j0:j1], in_=decay[:, t, j0:j1], func=ACT.Ln, bias=1.0)
+            nc.vector.scalar_tensor_tensor(
+                out=result[:, t, j0:j1],
+                in0=logs[:, t, j0:j1],
+                scalar=best[t][:],
+                in1=linear[:, t, j0:j1],
+                op0=ALU.add,
+                op1=ALU.add,
+            )
+            nc.sync.dma_start(out=out[t * P : (t + 1) * P, j0:j1], in_=result[:, t, j0:j1])

@@ -24,7 +24,8 @@ TILES = T // P
 QUADRANTS = 4
 LINE = 4
 
-PIECES = ((0, 0, 256, 208), (1, 0, 256, 208), (0, 256, 256, 208), (1, 256, 256, 208), (0, 512, 256, 208), (1, 512, 256, 192), (0, 768, 128, 128), (1, 768, 128, 128), (0, 896, 128, 128), (1, 896, 128, 64))
+LOADS = ((0, 0, 512), (1, 0, 512), (0, 512, 256), (1, 512, 256), (0, 768, 256), (1, 768, 128), (1, 896, 128))
+PIECES = ((0, 0, 256, 128), (0, 256, 256, 128), (1, 0, 256, 128), (1, 256, 256, 128), (2, 512, 256, 128), (3, 512, 256, 128), (4, 768, 256, 256), (5, 768, 128, 128), (6, 896, 128, 128))
 BLOCKS = ((0, 256), (256, 256), (512, 256), (768, 128), (896, 128))
 GATHERS = ((0, 0, 512), (1, 0, 256), (1, 256, 512))
 OUTS = ((0, 0, 256), (0, 256, 512), (1, 0, 256), (1, 256, 512))
@@ -57,7 +58,7 @@ def tile_list_runner_up_gap_kernel(tc, xt_words, xt_scales, wc, xs_words, xs_sca
             nc.vector.memset(plane[:].bitcast(U32), 0)
 
         raw = []
-        for n, (g, c0, width, share) in enumerate(PIECES):
+        for n, (g, c0, width) in enumerate(LOADS):
             piece = keep.tile([P, PACK, width], F32, name="raw%d" % n)
             rows = wc[g * K_PASS : (g + 1) * K_PASS, c0 : c0 + width]
             nc.sync.dma_start(out=piece[:], in_=rows.rearrange("(p j) c -> p j c", j=PACK))
@@ -82,20 +83,22 @@ def tile_list_runner_up_gap_kernel(tc, xt_words, xt_scales, wc, xs_words, xs_sca
         grouped = {}
 
         def cast(n):
-            g, c0, width, share = PIECES[n]
+            load, c0, width, share = PIECES[n]
+            shift = c0 - LOADS[load][1]
             grouped[n] = keep.tile([P, width, PACK], BF16, name="grouped%d" % n, align_bytes=64)
             for first, last, on_scalar in ((0, share, True), (share, width, False)):
                 if first == last:
                     continue
                 dst = grouped[n][:, first:last, :].rearrange("p (c i) j -> p c j i", i=LINE)
-                src = raw[n][:, :, first:last].rearrange("p j (c i) -> p c j i", i=LINE)
+                src = raw[load][:, :, shift + first : shift + last].rearrange("p j (c i) -> p c j i", i=LINE)
                 if on_scalar:
                     nc.scalar.activation(out=dst, in_=src, func=ACT.Copy)
                 else:
                     nc.vector.tensor_copy(out=dst, in_=src)
 
         def multiply(n):
-            g, c0, width, share = PIECES[n]
+            load, c0, width, share = PIECES[n]
+            g = LOADS[load][0]
             codes = keep.tile([P, width], U32, name="codes%d" % n, align_bytes=64)
             plane = keep.tile([P, width], U8, name="plane%d" % n, align_bytes=64)
             nc.vector.quantize_mx(
@@ -125,7 +128,8 @@ def tile_list_runner_up_gap_kernel(tc, xt_words, xt_scales, wc, xs_words, xs_sca
                     )
 
         def empty(n):
-            g, c0, width, share = PIECES[n]
+            load, c0, width, share = PIECES[n]
+            g = LOADS[load][0]
             if g != PASSES - 1:
                 return
             for b0, bw in BLOCKS:
@@ -144,14 +148,29 @@ def tile_list_runner_up_gap_kernel(tc, xt_words, xt_scales, wc, xs_words, xs_sca
                     )
                     best[t] = running
 
-        count = len(PIECES)
-        for n in range(count):
-            cast(n)
-            multiply(n)
-            if 1 <= n < count - 2:
-                empty(n - 1)
-        empty(count - 3)
-        empty(count - 1)
+        cast(0)
+        multiply(0)
+        cast(1)
+        multiply(1)
+        cast(2)
+        multiply(2)
+        cast(3)
+        multiply(3)
+        empty(2)
+        cast(4)
+        multiply(4)
+        empty(3)
+        cast(5)
+        multiply(5)
+        cast(6)
+        multiply(6)
+        empty(5)
+        cast(7)
+        multiply(7)
+        cast(8)
+        multiply(8)
+        empty(7)
+        empty(8)
 
         s = [spsum.tile([P, J], F32, name="s%d" % t, tag="late%d" % t) for t in range(TILES)]
         for t in range(TILES):

@@ -22,157 +22,125 @@ K_PASS = P * PACK
 PASSES = K // K_PASS
 TILES = T // P
 QUADRANTS = 4
-LINE = 4
+LIST_ROWS = 16
+MX_ALIGN = 64
+RUN = 4
 
-LOADS = ((0, 0, 512), (1, 0, 512), (0, 512, 256), (1, 512, 256), (0, 768, 256), (1, 768, 128), (1, 896, 128))
-PIECES = ((0, 0, 256, 128), (0, 256, 256, 128), (1, 0, 256, 128), (1, 256, 256, 128), (2, 512, 256, 128), (3, 512, 256, 128), (4, 768, 256, 256), (5, 768, 128, 128), (6, 896, 128, 128))
-BLOCKS = ((0, 256), (256, 256), (512, 256), (768, 128), (896, 128))
-GATHERS = ((0, 0, 512), (1, 0, 256), (1, 256, 512))
-OUTS = ((0, 0, 256), (0, 256, 512), (1, 0, 256), (1, 256, 512))
+BAND = 256
+BANDS = C // BAND
+LAST_PIECE = 128
+LAST_GATHER = 128
+OUT_PIECE = 256
 
 
-def load_scale_rows(queue, plane, scales):
+def wc_pieces():
+    pieces = []
+    for band in range(BANDS):
+        width = LAST_PIECE if band == BANDS - 1 else BAND
+        for first in range(band * BAND, (band + 1) * BAND, width):
+            for g in range(PASSES):
+                pieces.append((g, first, width))
+    return pieces
+
+
+def load_plane(nc, plane, scales):
     for q in range(QUADRANTS):
-        queue.dma_start(
+        nc.sync.dma_start(
             out=plane[32 * q : 32 * q + 4, :, :].bitcast(I32),
-            in_=scales[:, 4 * q : 4 * q + 4, :].rearrange("z r c -> r z c").bitcast(I32),
+            in_=scales[:, 4 * q : 4 * q + 4, :].rearrange("g r c -> r g c").bitcast(I32),
         )
 
 
 def tile_list_runner_up_gap_kernel(tc, xt_words, xt_scales, wc, xs_words, xs_scales, ws_words, ws_scales, offs, out):
     nc = tc.nc
+    pieces = wc_pieces()
     with ExitStack() as ctx:
         keep = ctx.enter_context(tc.tile_pool(name="keep", bufs=1))
-        zpsum = ctx.enter_context(tc.psum_pool(name="zpsum", bufs=3))
-        spsum = ctx.enter_context(tc.psum_pool(name="spsum", bufs=1))
+        psum = ctx.enter_context(tc.psum_pool(name="psum", bufs=1))
 
-        offsets = keep.tile([P, J // 16], U16, name="offsets")
-        xt_codes = keep.tile([P, PASSES, T], U32, name="xt_codes", align_bytes=64)
-        xt_plane = keep.tile([P, PASSES, T], U8, name="xt_plane", align_bytes=64)
-        xs_codes = keep.tile([P, 2 * T], U8, name="xs_codes", align_bytes=64)
-        xs_plane = keep.tile([P, 1, T], U8, name="xs_plane", align_bytes=64)
-        ws_codes = keep.tile([P, J], U32, name="ws_codes", align_bytes=64)
-        ws_plane = keep.tile([P, 1, J], U8, name="ws_plane", align_bytes=64)
+        offsets = keep.tile([P, J // LIST_ROWS], U16, name="offsets")
+        xt_codes = keep.tile([P, PASSES, T], U32, name="xt_codes", align_bytes=MX_ALIGN)
+        xt_plane = keep.tile([P, PASSES, T], U8, name="xt_plane", align_bytes=MX_ALIGN)
+        xs_codes = keep.tile([P, 2 * T], U8, name="xs_codes", align_bytes=MX_ALIGN)
+        xs_plane = keep.tile([P, 1, T], U8, name="xs_plane", align_bytes=MX_ALIGN)
+        ws_codes = keep.tile([P, J], U32, name="ws_codes", align_bytes=MX_ALIGN)
+        ws_plane = keep.tile([P, 1, J], U8, name="ws_plane", align_bytes=MX_ALIGN)
+
         nc.gpsimd.memset(xt_plane[:].bitcast(U32), 0)
-        for plane in (xs_plane, ws_plane):
-            nc.vector.memset(plane[:].bitcast(U32), 0)
+        nc.vector.memset(xs_plane[:].bitcast(U32), 0)
+        nc.vector.memset(ws_plane[:].bitcast(U32), 0)
 
         raw = []
-        for n, (g, c0, width) in enumerate(LOADS):
-            piece = keep.tile([P, PACK, width], F32, name="raw%d" % n)
-            rows = wc[g * K_PASS : (g + 1) * K_PASS, c0 : c0 + width]
-            nc.sync.dma_start(out=piece[:], in_=rows.rearrange("(p j) c -> p j c", j=PACK))
-            raw.append(piece)
+        for n, (g, first, width) in enumerate(pieces):
+            rows = wc[g * K_PASS : (g + 1) * K_PASS, first : first + width]
+            raw.append(keep.tile([P, PACK, width], F32, name="raw%d" % n))
+            nc.sync.dma_start(out=raw[n][:], in_=rows.rearrange("(p j) c -> p j c", j=PACK))
             if n == 0:
-                load_scale_rows(nc.sync, xt_plane, xt_scales)
+                load_plane(nc, xt_plane, xt_scales)
+            if n == PASSES - 1:
                 nc.sync.dma_start(
-                    out=xt_codes[:].bitcast(I32),
-                    in_=xt_words.rearrange("z p c r -> p z (c r)").bitcast(I32),
+                    out=xt_codes[:].bitcast(I32), in_=xt_words.rearrange("g p c j -> p g (c j)").bitcast(I32)
                 )
         nc.sync.dma_start(offsets[:], offs)
-        nc.sync.dma_start(
-            out=ws_codes[:].bitcast(I32), in_=ws_words[0].rearrange("p c r -> p (c r)").bitcast(I32)
-        )
+        nc.sync.dma_start(out=ws_codes[:].bitcast(I32), in_=ws_words[0].rearrange("p c j -> p (c j)").bitcast(I32))
         nc.sync.dma_start(out=xs_codes[:].bitcast(I32), in_=xs_words[0].bitcast(I32))
-        load_scale_rows(nc.sync, ws_plane, ws_scales)
-        load_scale_rows(nc.sync, xs_plane, xs_scales)
+        load_plane(nc, ws_plane, ws_scales)
+        load_plane(nc, xs_plane, xs_scales)
 
         z = [keep.tile([P, C], F32, name="z%d" % t) for t in range(TILES)]
+        banks = [[psum.tile([P, BAND], F32, name="bank%d_%d" % (band, t)) for t in range(TILES)] for band in range(BANDS)]
         best = [None] * TILES
-        banks = {}
-        grouped = {}
-
-        def cast(n):
-            load, c0, width, share = PIECES[n]
-            shift = c0 - LOADS[load][1]
-            grouped[n] = keep.tile([P, width, PACK], BF16, name="grouped%d" % n, align_bytes=64)
-            for first, last, on_scalar in ((0, share, True), (share, width, False)):
-                if first == last:
-                    continue
-                dst = grouped[n][:, first:last, :].rearrange("p (c i) j -> p c j i", i=LINE)
-                src = raw[load][:, :, shift + first : shift + last].rearrange("p j (c i) -> p c j i", i=LINE)
-                if on_scalar:
-                    nc.scalar.activation(out=dst, in_=src, func=ACT.Copy)
-                else:
-                    nc.vector.tensor_copy(out=dst, in_=src)
 
         def multiply(n):
-            load, c0, width, share = PIECES[n]
-            g = LOADS[load][0]
-            codes = keep.tile([P, width], U32, name="codes%d" % n, align_bytes=64)
-            plane = keep.tile([P, width], U8, name="plane%d" % n, align_bytes=64)
+            g, first, width = pieces[n]
+            band = first // BAND
+            grouped = keep.tile([P, width, PACK], BF16, name="grouped%d" % n, align_bytes=MX_ALIGN)
+            split = width // 2 if g == 0 or band == 0 else width
+            packed = grouped[:].rearrange("p (c i) j -> p c j i", i=RUN)
+            by_row = raw[n][:].rearrange("p j (c i) -> p c j i", i=RUN)
+            nc.scalar.activation(out=packed[:, : split // RUN], in_=by_row[:, : split // RUN], func=ACT.Copy)
+            if split < width:
+                nc.vector.tensor_copy(out=packed[:, split // RUN :], in_=by_row[:, split // RUN :])
+
+            codes = keep.tile([P, width], U32, name="codes%d" % n, align_bytes=MX_ALIGN)
+            plane = keep.tile([P, width], U8, name="plane%d" % n, align_bytes=MX_ALIGN)
             nc.vector.quantize_mx(
-                out=codes[:].bitcast(FP8X4),
-                scales=plane[:],
-                in_=grouped[n][:].rearrange("p c j -> p (c j)"),
+                out=codes[:].bitcast(FP8X4), scales=plane[:], in_=grouped[:].rearrange("p c j -> p (c j)")
             )
-            for b0, bw in BLOCKS:
-                if b0 < c0 or b0 + bw > c0 + width:
-                    continue
-                for t in range(TILES):
-                    if g == 0:
-                        if b0 + bw == C:
-                            banks[b0, t] = spsum.tile([P, bw], F32, name="last%d" % t, tag="late%d" % t)
-                        else:
-                            banks[b0, t] = zpsum.tile([P, bw], F32, name="zbank%d" % t)
-                    cols = slice(b0 - c0, b0 - c0 + bw)
-                    tokens = slice(t * P, (t + 1) * P)
-                    nc.tensor.matmul_mx(
-                        out=banks[b0, t][:],
-                        lhsT=xt_codes[:, g, tokens].bitcast(FP8X4),
-                        lhsT_scale=xt_plane[:, g, tokens],
-                        rhs=codes[:, cols].bitcast(FP8X4),
-                        rhs_scale=plane[:, cols],
-                        start=(g == 0),
-                        stop=(g == PASSES - 1),
-                    )
+            within = first - band * BAND
+            for t in range(TILES):
+                tokens = slice(t * P, (t + 1) * P)
+                nc.tensor.matmul_mx(
+                    out=banks[band][t][:, within : within + width],
+                    lhsT=xt_codes[:, g, tokens].bitcast(FP8X4),
+                    lhsT_scale=xt_plane[:, g, tokens],
+                    rhs=codes[:].bitcast(FP8X4),
+                    rhs_scale=plane[:],
+                    start=(g == 0 and within == 0),
+                    stop=(g == PASSES - 1 and within + width == BAND),
+                )
 
-        def empty(n):
-            load, c0, width, share = PIECES[n]
-            g = LOADS[load][0]
-            if g != PASSES - 1:
-                return
-            for b0, bw in BLOCKS:
-                if b0 < c0 or b0 + bw > c0 + width:
-                    continue
-                for t in range(TILES):
-                    running = keep.tile([P, 1], F32, name="best%d_%d" % (b0, t))
-                    nc.vector.tensor_scalar(
-                        out=z[t][:, b0 : b0 + bw],
-                        in0=banks[b0, t][:],
-                        scalar1=1.0,
-                        scalar2=None if best[t] is None else best[t][:],
-                        op0=ALU.mult,
-                        op1=ALU.max,
-                        accum_out=running[:],
-                    )
-                    best[t] = running
+        def empty(band):
+            for t in range(TILES):
+                running = keep.tile([P, 1], F32, name="best%d_%d" % (band, t))
+                nc.vector.tensor_scalar(
+                    out=z[t][:, band * BAND : (band + 1) * BAND],
+                    in0=banks[band][t][:],
+                    scalar1=1.0,
+                    scalar2=None if band == 0 else best[t][:],
+                    op0=ALU.mult,
+                    op1=ALU.max,
+                    accum_out=running[:],
+                )
+                best[t] = running
 
-        cast(0)
-        multiply(0)
-        cast(1)
-        multiply(1)
-        cast(2)
-        multiply(2)
-        cast(3)
-        multiply(3)
-        empty(2)
-        cast(4)
-        multiply(4)
-        empty(3)
-        cast(5)
-        multiply(5)
-        cast(6)
-        multiply(6)
-        empty(5)
-        cast(7)
-        multiply(7)
-        cast(8)
-        multiply(8)
-        empty(7)
-        empty(8)
+        for n, (g, first, width) in enumerate(pieces):
+            multiply(n)
+            if g == 0 and first > 0 and first % BAND == 0:
+                empty(first // BAND - 1)
+        empty(BANDS - 1)
 
-        s = [spsum.tile([P, J], F32, name="s%d" % t, tag="late%d" % t) for t in range(TILES)]
+        s = [psum.tile([P, J], F32, name="s%d" % t, tag="bank%d_%d" % (BANDS - 1, t)) for t in range(TILES)]
         for t in range(TILES):
             nc.tensor.matmul_mx(
                 out=s[t][:],
@@ -191,24 +159,29 @@ def tile_list_runner_up_gap_kernel(tc, xt_words, xt_scales, wc, xs_words, xs_sca
         result = keep.tile([P, TILES, J], F32, name="result")
         for t in range(TILES):
             nc.scalar.activation(out=negated[:, t : t + 1], in_=best[t][:], func=ACT.Copy, scale=-1.0)
-        for t, j0, j1 in GATHERS:
-            nc.vector.tensor_copy(picked[:, t, j0:j1], z[t][:].indirect(offsets[:, j0 // 16 : j1 // 16]))
-            nc.scalar.activation(
-                out=decay[:, t, j0:j1], in_=picked[:, t, j0:j1], func=ACT.Exp, bias=negated[:, t : t + 1]
-            )
+        for t in range(TILES):
+            cuts = (0, J - LAST_GATHER, J) if t == TILES - 1 else (0, J)
+            for j0, j1 in zip(cuts, cuts[1:]):
+                listed = offsets[:, j0 // LIST_ROWS : j1 // LIST_ROWS]
+                nc.vector.tensor_copy(picked[:, t, j0:j1], z[t][:].indirect(listed))
+                nc.scalar.activation(
+                    out=decay[:, t, j0:j1], in_=picked[:, t, j0:j1], func=ACT.Exp, bias=negated[:, t : t + 1]
+                )
         for t in range(TILES):
             nc.vector.scalar_tensor_tensor(
                 out=linear[:, t, :], in0=s[t][:], scalar=-0.5, in1=picked[:, t, :], op0=ALU.mult, op1=ALU.subtract
             )
         logs = keep.tile([P, TILES, J], F32, name="logs", tag="handover")
-        for t, j0, j1 in OUTS:
-            nc.scalar.activation(out=logs[:, t, j0:j1], in_=decay[:, t, j0:j1], func=ACT.Ln, bias=1.0)
-            nc.vector.scalar_tensor_tensor(
-                out=result[:, t, j0:j1],
-                in0=logs[:, t, j0:j1],
-                scalar=best[t][:],
-                in1=linear[:, t, j0:j1],
-                op0=ALU.add,
-                op1=ALU.add,
-            )
-            nc.sync.dma_start(out=out[t * P : (t + 1) * P, j0:j1], in_=result[:, t, j0:j1])
+        for t in range(TILES):
+            for j0 in range(0, J, OUT_PIECE):
+                columns = slice(j0, j0 + OUT_PIECE)
+                nc.scalar.activation(out=logs[:, t, columns], in_=decay[:, t, columns], func=ACT.Ln, bias=1.0)
+                nc.vector.scalar_tensor_tensor(
+                    out=result[:, t, columns],
+                    in0=logs[:, t, columns],
+                    scalar=best[t][:],
+                    in1=linear[:, t, columns],
+                    op0=ALU.add,
+                    op1=ALU.add,
+                )
+                nc.sync.dma_start(out=out[t * P : (t + 1) * P, columns], in_=result[:, t, columns])

@@ -26,21 +26,12 @@ LIST_ROWS = 16
 MX_ALIGN = 64
 RUN = 4
 
-BAND = 256
-BANDS = C // BAND
-LAST_PIECE = 128
+WIDTHS = (256, 256, 256, 128, 128)
+BANDS = len(WIDTHS)
+STARTS = [sum(WIDTHS[:band]) for band in range(BANDS)]
+BANK_SETS = 4
 LAST_GATHER = 128
 OUT_PIECE = 256
-
-
-def wc_pieces():
-    pieces = []
-    for band in range(BANDS):
-        width = LAST_PIECE if band == BANDS - 1 else BAND
-        for first in range(band * BAND, (band + 1) * BAND, width):
-            for g in range(PASSES):
-                pieces.append((g, first, width))
-    return pieces
 
 
 def load_plane(nc, plane, scales):
@@ -53,7 +44,7 @@ def load_plane(nc, plane, scales):
 
 def tile_list_runner_up_gap_kernel(tc, xt_words, xt_scales, wc, xs_words, xs_scales, ws_words, ws_scales, offs, out):
     nc = tc.nc
-    pieces = wc_pieces()
+    pieces = [(band, g) for band in range(BANDS) for g in range(PASSES)]
     with ExitStack() as ctx:
         keep = ctx.enter_context(tc.tile_pool(name="keep", bufs=1))
         psum = ctx.enter_context(tc.psum_pool(name="psum", bufs=1))
@@ -71,9 +62,9 @@ def tile_list_runner_up_gap_kernel(tc, xt_words, xt_scales, wc, xs_words, xs_sca
         nc.vector.memset(ws_plane[:].bitcast(U32), 0)
 
         raw = []
-        for n, (g, first, width) in enumerate(pieces):
-            rows = wc[g * K_PASS : (g + 1) * K_PASS, first : first + width]
-            raw.append(keep.tile([P, PACK, width], F32, name="raw%d" % n))
+        for n, (band, g) in enumerate(pieces):
+            rows = wc[g * K_PASS : (g + 1) * K_PASS, STARTS[band] : STARTS[band] + WIDTHS[band]]
+            raw.append(keep.tile([P, PACK, WIDTHS[band]], F32, name="raw%d" % n))
             nc.sync.dma_start(out=raw[n][:], in_=rows.rearrange("(p j) c -> p j c", j=PACK))
             if n == 0:
                 load_plane(nc, xt_plane, xt_scales)
@@ -82,24 +73,28 @@ def tile_list_runner_up_gap_kernel(tc, xt_words, xt_scales, wc, xs_words, xs_sca
                     out=xt_codes[:].bitcast(I32), in_=xt_words.rearrange("g p c j -> p g (c j)").bitcast(I32)
                 )
         nc.sync.dma_start(offsets[:], offs)
+        load_plane(nc, ws_plane, ws_scales)
         nc.sync.dma_start(out=ws_codes[:].bitcast(I32), in_=ws_words[0].rearrange("p c j -> p (c j)").bitcast(I32))
         nc.sync.dma_start(out=xs_codes[:].bitcast(I32), in_=xs_words[0].bitcast(I32))
-        load_plane(nc, ws_plane, ws_scales)
         load_plane(nc, xs_plane, xs_scales)
 
         z = [keep.tile([P, C], F32, name="z%d" % t) for t in range(TILES)]
-        banks = [[psum.tile([P, BAND], F32, name="bank%d_%d" % (band, t)) for t in range(TILES)] for band in range(BANDS)]
+        banks = {}
         best = [None] * TILES
 
+        def bank_tag(band, t):
+            return "bank%d_%d" % (BANK_SETS - 1 if band == BANDS - 1 else band % (BANK_SETS - 1), t)
+
         def multiply(n):
-            g, first, width = pieces[n]
-            band = first // BAND
+            band, g = pieces[n]
+            width = WIDTHS[band]
             grouped = keep.tile([P, width, PACK], BF16, name="grouped%d" % n, align_bytes=MX_ALIGN)
-            split = width // 2 if g == 0 or band == 0 else width
+            alone = band == BANDS - 1 or (g == 1 and band > 0 and width == max(WIDTHS))
+            split = width if alone else width // 2
             packed = grouped[:].rearrange("p (c i) j -> p c j i", i=RUN)
             by_row = raw[n][:].rearrange("p j (c i) -> p c j i", i=RUN)
             nc.scalar.activation(out=packed[:, : split // RUN], in_=by_row[:, : split // RUN], func=ACT.Copy)
-            if split < width:
+            if not alone:
                 nc.vector.tensor_copy(out=packed[:, split // RUN :], in_=by_row[:, split // RUN :])
 
             codes = keep.tile([P, width], U32, name="codes%d" % n, align_bytes=MX_ALIGN)
@@ -107,40 +102,42 @@ def tile_list_runner_up_gap_kernel(tc, xt_words, xt_scales, wc, xs_words, xs_sca
             nc.vector.quantize_mx(
                 out=codes[:].bitcast(FP8X4), scales=plane[:], in_=grouped[:].rearrange("p c j -> p (c j)")
             )
-            within = first - band * BAND
             for t in range(TILES):
+                if g == 0:
+                    banks[band, t] = psum.tile([P, width], F32, name="z_sum%d_%d" % (band, t), tag=bank_tag(band, t))
                 tokens = slice(t * P, (t + 1) * P)
                 nc.tensor.matmul_mx(
-                    out=banks[band][t][:, within : within + width],
+                    out=banks[band, t][:],
                     lhsT=xt_codes[:, g, tokens].bitcast(FP8X4),
                     lhsT_scale=xt_plane[:, g, tokens],
                     rhs=codes[:].bitcast(FP8X4),
                     rhs_scale=plane[:],
-                    start=(g == 0 and within == 0),
-                    stop=(g == PASSES - 1 and within + width == BAND),
+                    start=(g == 0),
+                    stop=(g == PASSES - 1),
                 )
 
-        def empty(band):
+        def empty(band, tag):
+            running = keep.tile([P, TILES], F32, name="best%d" % band, tag=tag, align_bytes=MX_ALIGN)
             for t in range(TILES):
-                running = keep.tile([P, 1], F32, name="best%d_%d" % (band, t))
                 nc.vector.tensor_scalar(
-                    out=z[t][:, band * BAND : (band + 1) * BAND],
-                    in0=banks[band][t][:],
+                    out=z[t][:, STARTS[band] : STARTS[band] + WIDTHS[band]],
+                    in0=banks[band, t][:],
                     scalar1=1.0,
-                    scalar2=None if band == 0 else best[t][:],
+                    scalar2=None if band == 0 else best[t],
                     op0=ALU.mult,
                     op1=ALU.max,
-                    accum_out=running[:],
+                    accum_out=running[:, t : t + 1],
                 )
-                best[t] = running
+                best[t] = running[:, t : t + 1]
 
-        for n, (g, first, width) in enumerate(pieces):
+        for n, (band, g) in enumerate(pieces):
             multiply(n)
-            if g == 0 and first > 0 and first % BAND == 0:
-                empty(first // BAND - 1)
-        empty(BANDS - 1)
+            if g == 0 and 0 < band < BANDS - 1:
+                empty(band - 1, "best%d" % (band - 1))
+        empty(BANDS - 2, "grouped%d" % (len(pieces) - 1))
+        empty(BANDS - 1, "best%d" % (BANDS - 1))
 
-        s = [psum.tile([P, J], F32, name="s%d" % t, tag="bank%d_%d" % (BANDS - 1, t)) for t in range(TILES)]
+        s = [psum.tile([P, J], F32, name="s%d" % t, tag=bank_tag(BANDS - 1, t)) for t in range(TILES)]
         for t in range(TILES):
             nc.tensor.matmul_mx(
                 out=s[t][:],
@@ -158,7 +155,7 @@ def tile_list_runner_up_gap_kernel(tc, xt_words, xt_scales, wc, xs_words, xs_sca
         linear = keep.tile([P, TILES, J], F32, name="linear")
         result = keep.tile([P, TILES, J], F32, name="result")
         for t in range(TILES):
-            nc.scalar.activation(out=negated[:, t : t + 1], in_=best[t][:], func=ACT.Copy, scale=-1.0)
+            nc.scalar.activation(out=negated[:, t : t + 1], in_=best[t], func=ACT.Copy, scale=-1.0)
         for t in range(TILES):
             cuts = (0, J - LAST_GATHER, J) if t == TILES - 1 else (0, J)
             for j0, j1 in zip(cuts, cuts[1:]):
@@ -179,7 +176,7 @@ def tile_list_runner_up_gap_kernel(tc, xt_words, xt_scales, wc, xs_words, xs_sca
                 nc.vector.scalar_tensor_tensor(
                     out=result[:, t, columns],
                     in0=logs[:, t, columns],
-                    scalar=best[t][:],
+                    scalar=best[t],
                     in1=linear[:, t, columns],
                     op0=ALU.add,
                     op1=ALU.add,

from contextlib import ExitStack

import concourse.mybir as mybir

K, L, T, C, J = 1024, 512, 256, 1024, 512
FLOPS = 2 * T * (K * C + L * J)

F32 = mybir.dt.float32
BF16 = mybir.dt.bfloat16
I32 = mybir.dt.int32
U32 = mybir.dt.uint32
U16 = mybir.dt.uint16
U8 = mybir.dt.uint8
FP8X4 = mybir.dt.float8_e4m3fn_x4
FP4X4 = mybir.dt.float4_e2m1fn_x4
ALU = mybir.AluOpType
ACT = mybir.ActivationFunctionType

P = 128
PACK = 4
K_PASS = P * PACK
PASSES = K // K_PASS
TILES = T // P
QUADRANTS = 4
LIST_ROWS = 16
MX_ALIGN = 64
RUN = 4

WIDTHS = (256, 256, 256, 128, 128)
BANDS = len(WIDTHS)
STARTS = [sum(WIDTHS[:band]) for band in range(BANDS)]
BANK_SETS = 4
LAST_GATHER = 128
OUT_PIECE = 256


def load_plane(nc, plane, scales):
    for q in range(QUADRANTS):
        nc.sync.dma_start(
            out=plane[32 * q : 32 * q + 4, :, :].bitcast(I32),
            in_=scales[:, 4 * q : 4 * q + 4, :].rearrange("g r c -> r g c").bitcast(I32),
        )


def tile_list_runner_up_gap_kernel(tc, xt_words, xt_scales, wc, xs_words, xs_scales, ws_words, ws_scales, offs, out):
    nc = tc.nc
    pieces = [(band, g) for band in range(BANDS) for g in range(PASSES)]
    with ExitStack() as ctx:
        keep = ctx.enter_context(tc.tile_pool(name="keep", bufs=1))
        psum = ctx.enter_context(tc.psum_pool(name="psum", bufs=1))

        offsets = keep.tile([P, J // LIST_ROWS], U16, name="offsets")
        xt_codes = keep.tile([P, PASSES, T], U32, name="xt_codes", align_bytes=MX_ALIGN)
        xt_plane = keep.tile([P, PASSES, T], U8, name="xt_plane", align_bytes=MX_ALIGN)
        xs_codes = keep.tile([P, 2 * T], U8, name="xs_codes", align_bytes=MX_ALIGN)
        xs_plane = keep.tile([P, 1, T], U8, name="xs_plane", align_bytes=MX_ALIGN)
        ws_codes = keep.tile([P, J], U32, name="ws_codes", align_bytes=MX_ALIGN)
        ws_plane = keep.tile([P, 1, J], U8, name="ws_plane", align_bytes=MX_ALIGN)

        nc.gpsimd.memset(xt_plane[:].bitcast(U32), 0)
        nc.vector.memset(xs_plane[:].bitcast(U32), 0)
        nc.vector.memset(ws_plane[:].bitcast(U32), 0)

        raw = []
        for n, (band, g) in enumerate(pieces):
            rows = wc[g * K_PASS : (g + 1) * K_PASS, STARTS[band] : STARTS[band] + WIDTHS[band]]
            raw.append(keep.tile([P, PACK, WIDTHS[band]], F32, name="raw%d" % n))
            nc.sync.dma_start(out=raw[n][:], in_=rows.rearrange("(p j) c -> p j c", j=PACK))
            if n == 0:
                load_plane(nc, xt_plane, xt_scales)
            if n == PASSES - 1:
                nc.sync.dma_start(
                    out=xt_codes[:].bitcast(I32), in_=xt_words.rearrange("g p c j -> p g (c j)").bitcast(I32)
                )
        nc.sync.dma_start(offsets[:], offs)
        load_plane(nc, ws_plane, ws_scales)
        nc.sync.dma_start(out=ws_codes[:].bitcast(I32), in_=ws_words[0].rearrange("p c j -> p (c j)").bitcast(I32))
        nc.sync.dma_start(out=xs_codes[:].bitcast(I32), in_=xs_words[0].bitcast(I32))
        load_plane(nc, xs_plane, xs_scales)

        z = [keep.tile([P, C], F32, name="z%d" % t) for t in range(TILES)]
        banks = {}
        best = [None] * TILES

        def bank_tag(band, t):
            return "bank%d_%d" % (BANK_SETS - 1 if band == BANDS - 1 else band % (BANK_SETS - 1), t)

        def multiply(n):
            band, g = pieces[n]
            width = WIDTHS[band]
            grouped = keep.tile([P, width, PACK], BF16, name="grouped%d" % n, align_bytes=MX_ALIGN)
            alone = band == BANDS - 1 or (g == 1 and band > 0 and width == max(WIDTHS))
            split = width if alone else width // 2
            packed = grouped[:].rearrange("p (c i) j -> p c j i", i=RUN)
            by_row = raw[n][:].rearrange("p j (c i) -> p c j i", i=RUN)
            nc.scalar.activation(out=packed[:, : split // RUN], in_=by_row[:, : split // RUN], func=ACT.Copy)
            if not alone:
                nc.vector.tensor_copy(out=packed[:, split // RUN :], in_=by_row[:, split // RUN :])

            codes = keep.tile([P, width], U32, name="codes%d" % n, align_bytes=MX_ALIGN)
            plane = keep.tile([P, width], U8, name="plane%d" % n, align_bytes=MX_ALIGN)
            nc.vector.quantize_mx(
                out=codes[:].bitcast(FP8X4), scales=plane[:], in_=grouped[:].rearrange("p c j -> p (c j)")
            )
            for t in range(TILES):
                if g == 0:
                    banks[band, t] = psum.tile([P, width], F32, name="z_sum%d_%d" % (band, t), tag=bank_tag(band, t))
                tokens = slice(t * P, (t + 1) * P)
                nc.tensor.matmul_mx(
                    out=banks[band, t][:],
                    lhsT=xt_codes[:, g, tokens].bitcast(FP8X4),
                    lhsT_scale=xt_plane[:, g, tokens],
                    rhs=codes[:].bitcast(FP8X4),
                    rhs_scale=plane[:],
                    start=(g == 0),
                    stop=(g == PASSES - 1),
                )

        def empty(band, tag):
            running = keep.tile([P, TILES], F32, name="best%d" % band, tag=tag, align_bytes=MX_ALIGN)
            for t in range(TILES):
                nc.vector.tensor_scalar(
                    out=z[t][:, STARTS[band] : STARTS[band] + WIDTHS[band]],
                    in0=banks[band, t][:],
                    scalar1=1.0,
                    scalar2=None if band == 0 else best[t],
                    op0=ALU.mult,
                    op1=ALU.max,
                    accum_out=running[:, t : t + 1],
                )
                best[t] = running[:, t : t + 1]

        for n, (band, g) in enumerate(pieces):
            multiply(n)
            if g == 0 and 0 < band < BANDS - 1:
                empty(band - 1, "best%d" % (band - 1))
        empty(BANDS - 2, "grouped%d" % (len(pieces) - 1))
        empty(BANDS - 1, "best%d" % (BANDS - 1))

        s = [psum.tile([P, J], F32, name="s%d" % t, tag=bank_tag(BANDS - 1, t)) for t in range(TILES)]
        for t in range(TILES):
            nc.tensor.matmul_mx(
                out=s[t][:],
                lhsT=xs_codes[:, 2 * t * P : 2 * (t + 1) * P].bitcast(FP4X4),
                lhsT_scale=xs_plane[:, 0, t * P : (t + 1) * P],
                rhs=ws_codes[:].bitcast(FP8X4),
                rhs_scale=ws_plane[:, 0, :],
                start=True,
                stop=True,
            )

        negated = keep.tile([P, TILES], F32, name="negated", tag="handover")
        picked = keep.tile([P, TILES, J], F32, name="picked")
        decay = keep.tile([P, TILES, J], F32, name="decay")
        linear = keep.tile([P, TILES, J], F32, name="linear")
        result = keep.tile([P, TILES, J], F32, name="result")
        for t in range(TILES):
            nc.scalar.activation(out=negated[:, t : t + 1], in_=best[t], func=ACT.Copy, scale=-1.0)
        for t in range(TILES):
            cuts = (0, J - LAST_GATHER, J) if t == TILES - 1 else (0, J)
            for j0, j1 in zip(cuts, cuts[1:]):
                listed = offsets[:, j0 // LIST_ROWS : j1 // LIST_ROWS]
                nc.vector.tensor_copy(picked[:, t, j0:j1], z[t][:].indirect(listed))
                nc.scalar.activation(
                    out=decay[:, t, j0:j1], in_=picked[:, t, j0:j1], func=ACT.Exp, bias=negated[:, t : t + 1]
                )
        for t in range(TILES):
            nc.vector.scalar_tensor_tensor(
                out=linear[:, t, :], in0=s[t][:], scalar=-0.5, in1=picked[:, t, :], op0=ALU.mult, op1=ALU.subtract
            )
        logs = keep.tile([P, TILES, J], F32, name="logs", tag="handover")
        for t in range(TILES):
            for j0 in range(0, J, OUT_PIECE):
                columns = slice(j0, j0 + OUT_PIECE)
                nc.scalar.activation(out=logs[:, t, columns], in_=decay[:, t, columns], func=ACT.Ln, bias=1.0)
                nc.vector.scalar_tensor_tensor(
                    out=result[:, t, columns],
                    in0=logs[:, t, columns],
                    scalar=best[t],
                    in1=linear[:, t, columns],
                    op0=ALU.add,
                    op1=ALU.add,
                )
                nc.sync.dma_start(out=out[t * P : (t + 1) * P, columns], in_=result[:, t, columns])
